import numpy as np
import ml_dtypes


def mxq(x, axis, fmt="e4m3"):
    dtype, down = {"e4m3": (ml_dtypes.float8_e4m3fn, 7), "e5m2": (ml_dtypes.float8_e5m2, 14)}[fmt]
    v = np.moveaxis(np.asarray(x, np.float32).astype(ml_dtypes.bfloat16).astype(np.float64), axis, -1)
    blocks = v.reshape(v.shape[:-1] + (-1, 32))
    amax = np.abs(blocks).max(-1, keepdims=True)
    byte = np.maximum(np.where(amax > 0, np.frexp(amax)[1] - 1 + 127, 0) - down, 1)
    scale = np.exp2(byte - 127.0)
    codes = (blocks / scale).astype(np.float32).astype(dtype).astype(np.float64)
    return np.moveaxis((codes * scale).reshape(v.shape), -1, axis)


WIDE = False


def mx_kscale(k):
    if not WIDE:
        return np.ones(k)
    levels = np.array([10, -10, 5, -5, 0])
    if k % 512:
        return np.exp2(np.random.permutation(np.resize(levels, k // 32))).repeat(32)
    a = np.empty((k // 512, 16))
    for p in range(k // 512):
        a[p, :8] = np.random.permutation(np.resize(levels, 8))
        for g in range(8):
            far = levels[np.abs(levels - a[p, g]) >= 10]
            a[p, g + 8] = far[np.random.randint(len(far))]
    return np.exp2(a.ravel()).repeat(32)


def f64(x):
    return np.asarray(x).astype(np.float64)


def striped(idx):
    return np.tile(np.asarray(idx).reshape(-1, 16).T, (8, 1)).astype(np.uint16)


def unstriped(offs):
    return offs[:16].T.reshape(-1).astype(np.int64)


def striped8(idx):
    return np.asarray(idx).reshape(8, -1, 16).transpose(0, 2, 1).reshape(128, -1).astype(np.uint16)


def unstriped8(offs):
    return offs.reshape(8, 16, -1).transpose(0, 2, 1).reshape(8, -1).astype(np.int64)


def pick8(x, idx, run):
    r = np.arange(len(x))
    return x[r[:, None], idx[r % (8 * run) // run]]


E2M1 = np.array([0.0, 0.5, 1.0, 1.5, 2.0, 3.0, 4.0, 6.0, -0.0, -0.5, -1.0, -1.5, -2.0, -3.0, -4.0, -6.0])


def pack_weight(w, fmt):
    k, n = w.shape
    w = f64(np.asarray(w, np.float32).astype(ml_dtypes.bfloat16)).reshape(k // 32, 32, n)
    amax = np.abs(w).max(1)
    if fmt == "e4m3":
        byte = np.frexp(amax)[1] - 1 + 127 - 7
    else:
        mant, ex = np.frexp(amax / 6.0)
        byte = np.where(mant > 0.5, ex, ex - 1) + 127
    byte = np.clip(np.where(amax > 0, byte, 1), 1, 254)
    scaled = (w * np.exp2(127.0 - byte)[:, None, :]).reshape(k, n).astype(np.float32)
    by_word = np.ascontiguousarray(scaled.reshape(k // 512, 128, 4, n).transpose(0, 1, 3, 2))
    if fmt == "e4m3":
        words = by_word.astype(ml_dtypes.float8_e4m3fn).view(np.uint8)
    else:
        c = by_word.astype(ml_dtypes.float4_e2m1fn).view(np.uint8) & 0xF
        words = (c[..., 0::2] | (c[..., 1::2] << 4)).reshape(k // 512, 128, 2 * n)
    return np.ascontiguousarray(words), np.ascontiguousarray(byte.astype(np.uint8).reshape(k // 512, 16, n))


def unpack_weight(words, scales, fmt):
    g, _, n = scales.shape
    words = np.ascontiguousarray(words).reshape(g, 128, n, -1)
    if fmt == "e4m3":
        vals = words.view(ml_dtypes.float8_e4m3fn).astype(np.float64)
    else:
        nib = np.empty((g, 128, n, 4), np.uint8)
        nib[..., 0::2] = words & 0xF
        nib[..., 1::2] = words >> 4
        vals = E2M1[nib]
    vals = vals * np.repeat(np.exp2(scales.astype(np.float64) - 127.0), 8, axis=1)[..., None]
    return vals.transpose(0, 1, 3, 2).reshape(g * 512, n)


K, J, R, T, Z, M, C, N, U = 512, 384, 512, 1024, 512, 1024, 512, 256, 1024


def setup_inputs():
    n = np.random.standard_normal
    idx = np.random.permutation(T)[:J]
    idx2 = np.random.permutation(M)[:J]
    idx3 = np.stack([np.random.permutation(C)[:J] for _ in range(8)])
    idx4 = np.stack([np.random.permutation(C)[:J] for _ in range(8)])
    idx5 = np.stack([np.random.permutation(U)[:C] for _ in range(8)])
    fk = mx_kscale(K)
    fr = mx_kscale(R)
    fz = mx_kscale(Z)
    xtp = pack_weight(n((K, T)) * fk[:, None], "e2m1")
    wp = pack_weight(n((K, R)) * 1 / np.sqrt(K) / fk[:, None] * fr, "e4m3")
    xop = pack_weight(n((Z, M)) / fz[:, None], "e2m1")
    w2p = pack_weight(n((Z, R)) * 1 / np.sqrt(Z) * fz[:, None] * fr, "e4m3")
    wbp = pack_weight(n((R, N)) * 1 / np.sqrt(R) / fr[:, None], "e4m3")
    return {
        "xt_words": xtp[0],
        "xt_scales": xtp[1],
        "w_words": wp[0],
        "w_scales": wp[1],
        "xo_words": xop[0],
        "xo_scales": xop[1],
        "w2_words": w2p[0],
        "w2_scales": w2p[1],
        "wb_words": wbp[0],
        "wb_scales": wbp[1],
        "offs": striped(idx),
        "offs2": striped(idx2),
        "offs3": striped8(idx3),
        "offs4": striped8(idx4),
        "offs5": striped8(idx5),
    }


def reference(xt_words, xt_scales, w_words, w_scales, xo_words, xo_scales, w2_words, w2_scales, wb_words, wb_scales, offs, offs2, offs3, offs4, offs5):
    idx = unstriped(offs)
    idx2 = unstriped(offs2)
    idx3 = unstriped8(offs3)
    idx4 = unstriped8(offs4)
    idx5 = unstriped8(offs5)
    xtu = unpack_weight(xt_words, xt_scales, "e2m1")
    wu = unpack_weight(w_words, w_scales, "e4m3")
    xou = unpack_weight(xo_words, xo_scales, "e2m1")
    w2u = unpack_weight(w2_words, w2_scales, "e4m3")
    wbu = unpack_weight(wb_words, wb_scales, "e4m3")
    xtidxg = xtu[:, idx]
    a = wu.T @ xtidxg
    xoidx2g = xou[:, idx2]
    b = w2u.T @ xoidx2g
    pw = np.zeros((R, C))
    pw[np.arange(R)[:, None], idx3[np.arange(R) % 512 // 64]] = a
    pv = np.zeros((R, C))
    pv[np.arange(R)[:, None], idx4[np.arange(R) % 512 // 64]] = b
    g0 = np.pad(pw, ((0, 0), (1, 0)))[:, :C]
    g1 = pw + g0
    g2 = np.pad(g1, ((0, 0), (2, 0)))[:, :C]
    g3 = g1 + g2
    hid = np.maximum(g3, pv)
    hidq = mxq(hid, 0, "e4m3")
    p = wbu.T @ hidq
    m0 = np.zeros((N, U))
    m0[np.arange(N)[:, None], idx5[np.arange(N) % 128 // 16]] = p
    m1 = np.pad(m0, ((0, 0), (1, 0)))[:, :U]
    y = m0 - m1
    return y

@@ -1,0 +1,220 @@
+from contextlib import ExitStack
+
+import concourse.mybir as mybir
+
+F32 = mybir.dt.float32
+BF16 = mybir.dt.bfloat16
+I32 = mybir.dt.int32
+U32 = mybir.dt.uint32
+U16 = mybir.dt.uint16
+U8 = mybir.dt.uint8
+FP8X4 = mybir.dt.float8_e4m3fn_x4
+FP4X4 = mybir.dt.float4_e2m1fn_x4
+ADD = mybir.AluOpType.add
+SUB = mybir.AluOpType.subtract
+MAX = mybir.AluOpType.max
+COPY = mybir.ActivationFunctionType.Copy
+
+P = 128
+PACK = 4
+J, R, T, C, N, U = 384, 512, 1024, 512, 256, 1024
+FIRST = 128
+C_CHUNKS = ((0, 64), (64, 128), (128, 256), (256, 512))
+U_CHUNKS = (((0, 512), (512, 1024)), ((0, 128), (128, 384), (384, 640), (640, 896), (896, 1024)))
+FLOPS = 2 * 512 * R * J * 2 + 2 * R * N * C
+
+
+def tile_picked_tokens_plain_two_trailing_one_endsteps_kernel(
+    tc, xt_words, xt_scales, w_words, w_scales, xo_words, xo_scales, w2_words, w2_scales,
+    wb_words, wb_scales, offs, offs2, offs3, offs4, offs5, out,
+):
+    nc = tc.nc
+    with ExitStack() as ctx:
+        lists = ctx.enter_context(tc.tile_pool(name="lists", bufs=1))
+        sb = ctx.enter_context(tc.tile_pool(name="sb", bufs=1))
+        ps = ctx.enter_context(tc.psum_pool(name="ps", bufs=1))
+
+        def new(shape, dtype, name, tag=None):
+            return sb.tile(shape, dtype, name=name, tag=tag or name, align_bytes=64)
+
+        def bank(index, width):
+            return ps.tile([P, width], F32, name="bank%d" % index)
+
+        def load_list(source, name):
+            tile = lists.tile(list(source.shape), U16, name=name)
+            nc.sync.dma_start(tile[:], source)
+            return tile
+
+        def load_fp4_words(source, name):
+            tile = new([P, T], U16, name)
+            nc.sync.dma_start(tile[:].bitcast(I32), source[0].bitcast(I32))
+            return tile
+
+        def load_fp8_words(source, name):
+            tile = new([P, source.shape[2]], U32, name)
+            nc.sync.dma_start(tile[:].bitcast(I32), source[0].rearrange("p n t -> p (n t)").bitcast(I32))
+            return tile
+
+        def cleared_plane(width, name):
+            tile = new([P, width], U8, name)
+            nc.vector.memset(tile[:].bitcast(I32), 0)
+            return tile
+
+        def load_scales(plane, source):
+            for q in range(4):
+                nc.sync.dma_start(plane[32 * q : 32 * q + 4, :].bitcast(I32), source[0, 4 * q : 4 * q + 4, :].bitcast(I32))
+
+        def cleared_board(engine, width, name, tag=None):
+            tile = new([P, width], F32, name, tag)
+            engine.memset(tile[:], 0.0)
+            return tile
+
+        def gather(window, dtype, offsets, lo, hi, name):
+            tile = new([P, hi - lo], dtype, name)
+            nc.vector.tensor_copy(tile[:], window[:].indirect(offsets[:, lo // 16 : hi // 16]))
+            return tile
+
+        def deal(source, dtype, lo, hi, name):
+            tile = new([P, hi - lo, P], dtype, name)
+            nc.vector.tensor_copy(tile[:], source[:].rearrange("p (m t) -> p t m", t=PACK)[:, lo:hi, :])
+            return tile
+
+        def product(acc, wt_words, wt_scales, moving, moving_scales, fmt):
+            nc.tensor.matmul_mx(out=acc, lhsT=wt_words.bitcast(FP8X4), lhsT_scale=wt_scales,
+                                rhs=moving.bitcast(fmt), rhs_scale=moving_scales, start=True, stop=True)
+
+        def scatter(board, offsets, lo, hi, values):
+            nc.scalar.activation(board[:].indirect(offsets[:, lo // 16 : hi // 16]), values, COPY)
+
+        xt_plane = cleared_plane(T, "xt_plane")
+        w_plane = cleared_plane(R, "w_plane")
+        xt_stage = new([P, 2, T // 4], I32, "xt_stage")
+        for half in range(2):
+            rows = xt_scales[0, 8 * half : 8 * half + 8, :].bitcast(I32)
+            nc.sync.dma_start(xt_stage[64 * half : 64 * half + 4, :, :], rows.rearrange("(q r) c -> r q c", r=4))
+        w_stage = new([4, 4, R // 4], I32, "w_stage")
+        nc.sync.dma_start(w_stage[:], w_scales[0].bitcast(I32).rearrange("(q r) c -> r q c", r=4))
+        l3 = load_list(offs3, "l3")
+        l1 = load_list(offs, "l1")
+        xt_w = load_fp4_words(xt_words, "xt_w")
+        w_w = load_fp8_words(w_words, "w_w")
+        pw = [cleared_board(nc.vector, C, "pw%d" % t) for t in range(PACK)]
+
+        xo_plane = cleared_plane(T, "xo_plane")
+        w2_plane = cleared_plane(R, "w2_plane")
+        wb_plane = cleared_plane(N, "wb_plane")
+        l2 = load_list(offs2, "l2")
+        xo_w = load_fp4_words(xo_words, "xo_w")
+        load_scales(xo_plane, xo_scales)
+        w2_w = load_fp8_words(w2_words, "w2_w")
+        load_scales(w2_plane, w2_scales)
+        l4 = load_list(offs4, "l4")
+        wb_w = load_fp8_words(wb_words, "wb_w")
+        load_scales(wb_plane, wb_scales)
+        l5 = load_list(offs5, "l5")
+
+        for q in range(4):
+            first = 64 * (q // 2)
+            nc.vector.tensor_copy(xt_plane[32 * q : 32 * q + 4, :].bitcast(I32), xt_stage[first : first + 4, q % 2, :])
+        for q in range(4):
+            nc.vector.tensor_copy(w_plane[32 * q : 32 * q + 4, :].bitcast(I32), w_stage[:, q, :])
+        xa_s = gather(xt_plane, U8, l1, 0, FIRST, "xa_s")
+        w_s0 = deal(w_plane, U8, 0, 1, "w_s0")
+        xa_w = gather(xt_w, U16, l1, 0, FIRST, "xa_w")
+        w_w0 = deal(w_w, U32, 0, 1, "w_w0")
+        acc = bank(0, FIRST)
+        product(acc[:], w_w0[:, 0, :], w_s0[:, 0, :], xa_w[:], xa_s[:], FP4X4)
+        a_first0 = new([P, FIRST], F32, "a_first0")
+        nc.vector.tensor_copy(a_first0[:], acc[:])
+        scatter(pw[0], l3, 0, FIRST, a_first0[:])
+
+        w_s1 = deal(w_plane, U8, 1, PACK, "w_s1")
+        w_w1 = deal(w_w, U32, 1, PACK, "w_w1")
+        wd = [w_w0[:, 0, :]] + [w_w1[:, t, :] for t in range(PACK - 1)]
+        sd = [w_s0[:, 0, :]] + [w_s1[:, t, :] for t in range(PACK - 1)]
+        acc = bank(1, (PACK - 1) * FIRST)
+        for t in range(1, PACK):
+            product(acc[:, (t - 1) * FIRST : t * FIRST], wd[t], sd[t], xa_w[:], xa_s[:], FP4X4)
+        a_first = new([P, (PACK - 1) * FIRST], F32, "a_first")
+        nc.vector.tensor_copy(a_first[:], acc[:])
+        for t in range(1, PACK):
+            scatter(pw[t], l3, 0, FIRST, a_first[:, (t - 1) * FIRST : t * FIRST])
+
+        rest = J - FIRST
+        xb_s = gather(xt_plane, U8, l1, FIRST, J, "xb_s")
+        xb_w = gather(xt_w, U16, l1, FIRST, J, "xb_w")
+        for half in range(2):
+            acc = bank(2 + half, 2 * rest)
+            for i in range(2):
+                t = 2 * half + i
+                product(acc[:, i * rest : (i + 1) * rest], wd[t], sd[t], xb_w[:], xb_s[:], FP4X4)
+            a_rest = new([P, 2 * rest], F32, "a_rest%d" % half)
+            nc.vector.tensor_copy(a_rest[:], acc[:])
+            for i in range(2):
+                scatter(pw[2 * half + i], l3, FIRST, J, a_rest[:, i * rest : (i + 1) * rest])
+
+        xo_gs = gather(xo_plane, U8, l2, 0, J, "xo_g_s")
+        xo_gw = gather(xo_w, U16, l2, 0, J, "xo_g_w")
+        w2_sd = deal(w2_plane, U8, 0, PACK, "w2_sd")
+        w2_wd = deal(w2_w, U32, 0, PACK, "w2_wd")
+        pv = [cleared_board(nc.gpsimd, C, "pv%d" % t, tag) for t, tag in enumerate(("xt_w", "xt_plane", "xo_w", "xo_plane"))]
+        for t in range(PACK):
+            acc = bank(4 + t, J)
+            for lo, hi in ((0, 256), (256, J)):
+                product(acc[:, lo:hi], w2_wd[:, t, :], w2_sd[:, t, :], xo_gw[:, lo:hi], xo_gs[:, lo:hi], FP4X4)
+            b_t = new([P, J], F32, "b%d" % t)
+            nc.vector.tensor_copy(b_t[:], acc[:])
+            scatter(pv[t], l4, 0, J, b_t[:])
+        m0 = [cleared_board(nc.gpsimd, U, "m0_%d" % j, tag) for j, tag in enumerate(("w2_w", "w2_plane"))]
+
+        g3 = []
+        for t in range(PACK):
+            g1 = new([P, 2 + C], F32, "g1_%d" % t, ("xo_g_w", "xo_g_s", "w2_wd", "w2_sd")[t])
+            nc.vector.memset(g1[:, 0:2], 0.0)
+            nc.vector.tensor_copy(g1[:, 2:3], pw[t][:, 0:1])
+            nc.vector.tensor_tensor(g1[:, 3 : 2 + C], pw[t][:, 1:C], pw[t][:, 0 : C - 1], ADD)
+            g3_t = new([P, C], F32, "g3_%d" % t)
+            nc.vector.tensor_tensor(g3_t[:], g1[:, 2 : 2 + C], g1[:, 0:C], ADD)
+            g3.append(g3_t)
+
+        last = PACK - 1
+        planes = new([P, last, C], BF16, "planes")
+        for t in range(last):
+            nc.vector.tensor_tensor(planes[:, t, :], g3[t][:], pv[t][:], MAX)
+        woven = [new([P, hi - lo, PACK], BF16, "woven%d" % k) for k, (lo, hi) in enumerate(C_CHUNKS)]
+        for k, (lo, hi) in enumerate(C_CHUNKS):
+            nc.vector.tensor_copy(woven[k][:, :, 0:last], planes[:, :, lo:hi].rearrange("p t c -> p c t"))
+
+        banks_used = 0
+        for k, (lo, hi) in enumerate(C_CHUNKS):
+            width = hi - lo
+            nc.vector.tensor_tensor(woven[k][:, :, last], g3[last][:, lo:hi], pv[last][:, lo:hi], MAX)
+            hid_w = new([P, width], U32, "hid_w%d" % k)
+            hid_s = new([P, width], U8, "hid_s%d" % k)
+            nc.vector.quantize_mx(out=hid_w[:].bitcast(FP8X4), scales=hid_s[:], in_=woven[k][:].rearrange("p c t -> p (c t)"))
+            groups = ((0,), (1,)) if width < P else ((0, 1),)
+            sources = []
+            for group in groups:
+                acc = bank(banks_used, len(group) * width)
+                banks_used = banks_used + 1
+                for i, j in enumerate(group):
+                    product(acc[:, i * width : (i + 1) * width], wb_w[:, j * P : (j + 1) * P],
+                            wb_plane[:, j * P : (j + 1) * P], hid_w[:], hid_s[:], FP8X4)
+                p_k = new([P, len(group) * width], F32, "p%d_%d" % (k, group[0]))
+                if k == 0:
+                    nc.scalar.copy(p_k[:], acc[:])
+                else:
+                    nc.vector.tensor_copy(p_k[:], acc[:])
+                sources.extend(p_k[:, i * width : (i + 1) * width] for i in range(len(group)))
+            for j in range(N // P):
+                scatter(m0[j], l5, lo, hi, sources[j])
+
+        for j in range(N // P):
+            for lo, hi in U_CHUNKS[j]:
+                y = new([P, hi - lo], F32, "y%d_%d" % (j, lo))
+                if lo == 0:
+                    nc.vector.tensor_copy(y[:, 0:1], m0[j][:, 0:1])
+                    nc.vector.tensor_tensor(y[:, 1:], m0[j][:, 1:hi], m0[j][:, 0 : hi - 1], SUB)
+                else:
+                    nc.vector.tensor_tensor(y[:], m0[j][:, lo:hi], m0[j][:, lo - 1 : hi - 1], SUB)
+                nc.sync.dma_start(out[j * P : (j + 1) * P, lo:hi], y[:])

@@ -66,7 +66,7 @@ def tile_picked_tokens_plain_two_trailing_one_endsteps_kernel(
 
         def cleared_board(engine, width, name, tag=None):
             tile = new([P, width], F32, name, tag)
-            engine.memset(tile[:], 0.0)
+            engine.memset(tile[:].bitcast(I32), 0)
             return tile
 
         def gather(window, dtype, offsets, lo, hi, name):
@@ -88,49 +88,31 @@ def tile_picked_tokens_plain_two_trailing_one_endsteps_kernel(
 
         xt_plane = cleared_plane(T, "xt_plane")
         w_plane = cleared_plane(R, "w_plane")
-        xt_stage = new([P, 2, T // 4], I32, "xt_stage")
-        for half in range(2):
-            rows = xt_scales[0, 8 * half : 8 * half + 8, :].bitcast(I32)
-            nc.sync.dma_start(xt_stage[64 * half : 64 * half + 4, :, :], rows.rearrange("(q r) c -> r q c", r=4))
         w_stage = new([4, 4, R // 4], I32, "w_stage")
         nc.sync.dma_start(w_stage[:], w_scales[0].bitcast(I32).rearrange("(q r) c -> r q c", r=4))
-        l3 = load_list(offs3, "l3")
         l1 = load_list(offs, "l1")
         xt_w = load_fp4_words(xt_words, "xt_w")
         w_w = load_fp8_words(w_words, "w_w")
-        pw = [cleared_board(nc.vector, C, "pw%d" % t) for t in range(PACK)]
+        load_scales(xt_plane, xt_scales)
+        l3 = load_list(offs3, "l3")
+        pw = [cleared_board(nc.vector, C, "pw0")]
 
-        xo_plane = cleared_plane(T, "xo_plane")
-        w2_plane = cleared_plane(R, "w2_plane")
-        wb_plane = cleared_plane(N, "wb_plane")
-        l2 = load_list(offs2, "l2")
-        xo_w = load_fp4_words(xo_words, "xo_w")
-        load_scales(xo_plane, xo_scales)
-        w2_w = load_fp8_words(w2_words, "w2_w")
-        load_scales(w2_plane, w2_scales)
-        l4 = load_list(offs4, "l4")
-        wb_w = load_fp8_words(wb_words, "wb_w")
-        load_scales(wb_plane, wb_scales)
-        l5 = load_list(offs5, "l5")
-
-        for q in range(4):
-            first = 64 * (q // 2)
-            nc.vector.tensor_copy(xt_plane[32 * q : 32 * q + 4, :].bitcast(I32), xt_stage[first : first + 4, q % 2, :])
         for q in range(4):
             nc.vector.tensor_copy(w_plane[32 * q : 32 * q + 4, :].bitcast(I32), w_stage[:, q, :])
-        xa_s = gather(xt_plane, U8, l1, 0, FIRST, "xa_s")
-        w_s0 = deal(w_plane, U8, 0, 1, "w_s0")
+        w_wd = new([P, PACK, P], U32, "w_wd")
+        nc.scalar.copy(w_wd[:].rearrange("p t m -> p m t"), w_w[:].rearrange("p (m t) -> p m t", t=PACK))
         xa_w = gather(xt_w, U16, l1, 0, FIRST, "xa_w")
-        w_w0 = deal(w_w, U32, 0, 1, "w_w0")
+        w_s0 = deal(w_plane, U8, 0, 1, "w_s0")
+        xa_s = gather(xt_plane, U8, l1, 0, FIRST, "xa_s")
         acc = bank(0, FIRST)
-        product(acc[:], w_w0[:, 0, :], w_s0[:, 0, :], xa_w[:], xa_s[:], FP4X4)
+        product(acc[:], w_wd[:, 0, :], w_s0[:, 0, :], xa_w[:], xa_s[:], FP4X4)
         a_first0 = new([P, FIRST], F32, "a_first0")
-        nc.vector.tensor_copy(a_first0[:], acc[:])
+        nc.scalar.copy(a_first0[:], acc[:])
         scatter(pw[0], l3, 0, FIRST, a_first0[:])
 
+        pw.extend(cleared_board(nc.vector, C, "pw%d" % t) for t in range(1, PACK))
         w_s1 = deal(w_plane, U8, 1, PACK, "w_s1")
-        w_w1 = deal(w_w, U32, 1, PACK, "w_w1")
-        wd = [w_w0[:, 0, :]] + [w_w1[:, t, :] for t in range(PACK - 1)]
+        wd = [w_wd[:, t, :] for t in range(PACK)]
         sd = [w_s0[:, 0, :]] + [w_s1[:, t, :] for t in range(PACK - 1)]
         acc = bank(1, (PACK - 1) * FIRST)
         for t in range(1, PACK):
@@ -152,6 +134,19 @@ def tile_picked_tokens_plain_two_trailing_one_endsteps_kernel(
             nc.vector.tensor_copy(a_rest[:], acc[:])
             for i in range(2):
                 scatter(pw[2 * half + i], l3, FIRST, J, a_rest[:, i * rest : (i + 1) * rest])
+
+        xo_plane = cleared_plane(T, "xo_plane")
+        w2_plane = cleared_plane(R, "w2_plane")
+        wb_plane = cleared_plane(N, "wb_plane")
+        l2 = load_list(offs2, "l2")
+        xo_w = load_fp4_words(xo_words, "xo_w")
+        load_scales(xo_plane, xo_scales)
+        w2_w = load_fp8_words(w2_words, "w2_w")
+        load_scales(w2_plane, w2_scales)
+        l4 = load_list(offs4, "l4")
+        wb_w = load_fp8_words(wb_words, "wb_w")
+        load_scales(wb_plane, wb_scales)
+        l5 = load_list(offs5, "l5")
 
         xo_gs = gather(xo_plane, U8, l2, 0, J, "xo_g_s")
         xo_gw = gather(xo_w, U16, l2, 0, J, "xo_g_w")
@@ -178,12 +173,10 @@ def tile_picked_tokens_plain_two_trailing_one_endsteps_kernel(
             g3.append(g3_t)
 
         last = PACK - 1
-        planes = new([P, last, C], BF16, "planes")
-        for t in range(last):
-            nc.vector.tensor_tensor(planes[:, t, :], g3[t][:], pv[t][:], MAX)
         woven = [new([P, hi - lo, PACK], BF16, "woven%d" % k) for k, (lo, hi) in enumerate(C_CHUNKS)]
-        for k, (lo, hi) in enumerate(C_CHUNKS):
-            nc.vector.tensor_copy(woven[k][:, :, 0:last], planes[:, :, lo:hi].rearrange("p t c -> p c t"))
+        for t in range(last):
+            for k, (lo, hi) in enumerate(C_CHUNKS):
+                nc.vector.tensor_tensor(woven[k][:, :, t], g3[t][:, lo:hi], pv[t][:, lo:hi], MAX)
 
         banks_used = 0
         for k, (lo, hi) in enumerate(C_CHUNKS):

@@ -55,9 +55,9 @@ def tile_picked_tokens_plain_two_trailing_one_endsteps_kernel(
             nc.sync.dma_start(tile[:].bitcast(I32), source[0].rearrange("p n t -> p (n t)").bitcast(I32))
             return tile
 
-        def cleared_plane(width, name):
-            tile = new([P, width], U8, name)
-            nc.vector.memset(tile[:].bitcast(I32), 0)
+        def cleared_plane(engine, width, name, tag=None):
+            tile = new([P, width], U8, name, tag)
+            engine.memset(tile[:].bitcast(I32), 0)
             return tile
 
         def load_scales(plane, source):
@@ -69,14 +69,14 @@ def tile_picked_tokens_plain_two_trailing_one_endsteps_kernel(
             engine.memset(tile[:].bitcast(I32), 0)
             return tile
 
-        def gather(window, dtype, offsets, lo, hi, name):
-            tile = new([P, hi - lo], dtype, name)
+        def gather(window, dtype, offsets, lo, hi, name, tag=None):
+            tile = new([P, hi - lo], dtype, name, tag)
             nc.vector.tensor_copy(tile[:], window[:].indirect(offsets[:, lo // 16 : hi // 16]))
             return tile
 
-        def deal(source, dtype, lo, hi, name):
-            tile = new([P, hi - lo, P], dtype, name)
-            nc.vector.tensor_copy(tile[:], source[:].rearrange("p (m t) -> p t m", t=PACK)[:, lo:hi, :])
+        def deal(source, dtype, name):
+            tile = new([P, PACK, P], dtype, name)
+            nc.vector.tensor_copy(tile[:], source[:].rearrange("p (m t) -> p t m", t=PACK))
             return tile
 
         def product(acc, wt_words, wt_scales, moving, moving_scales, fmt):
@@ -86,8 +86,8 @@ def tile_picked_tokens_plain_two_trailing_one_endsteps_kernel(
         def scatter(board, offsets, lo, hi, values):
             nc.scalar.activation(board[:].indirect(offsets[:, lo // 16 : hi // 16]), values, COPY)
 
-        xt_plane = cleared_plane(T, "xt_plane")
-        w_plane = cleared_plane(R, "w_plane")
+        xt_plane = cleared_plane(nc.vector, T, "xt_plane")
+        w_plane = cleared_plane(nc.vector, R, "w_plane")
         w_stage = new([4, 4, R // 4], I32, "w_stage")
         nc.sync.dma_start(w_stage[:], w_scales[0].bitcast(I32).rearrange("(q r) c -> r q c", r=4))
         l1 = load_list(offs, "l1")
@@ -95,49 +95,43 @@ def tile_picked_tokens_plain_two_trailing_one_endsteps_kernel(
         w_w = load_fp8_words(w_words, "w_w")
         load_scales(xt_plane, xt_scales)
         l3 = load_list(offs3, "l3")
-        pw = [cleared_board(nc.vector, C, "pw0")]
+        pw = [cleared_board(nc.vector, C, "pw%d" % t) for t in range(PACK - 1)]
 
         for q in range(4):
             nc.vector.tensor_copy(w_plane[32 * q : 32 * q + 4, :].bitcast(I32), w_stage[:, q, :])
         w_wd = new([P, PACK, P], U32, "w_wd")
         nc.scalar.copy(w_wd[:].rearrange("p t m -> p m t"), w_w[:].rearrange("p (m t) -> p m t", t=PACK))
+        w_sd = deal(w_plane, U8, "w_sd")
         xa_w = gather(xt_w, U16, l1, 0, FIRST, "xa_w")
-        w_s0 = deal(w_plane, U8, 0, 1, "w_s0")
         xa_s = gather(xt_plane, U8, l1, 0, FIRST, "xa_s")
         acc = bank(0, FIRST)
-        product(acc[:], w_wd[:, 0, :], w_s0[:, 0, :], xa_w[:], xa_s[:], FP4X4)
+        product(acc[:], w_wd[:, 0, :], w_sd[:, 0, :], xa_w[:], xa_s[:], FP4X4)
         a_first0 = new([P, FIRST], F32, "a_first0")
         nc.scalar.copy(a_first0[:], acc[:])
         scatter(pw[0], l3, 0, FIRST, a_first0[:])
 
-        pw.extend(cleared_board(nc.vector, C, "pw%d" % t) for t in range(1, PACK))
-        w_s1 = deal(w_plane, U8, 1, PACK, "w_s1")
-        wd = [w_wd[:, t, :] for t in range(PACK)]
-        sd = [w_s0[:, 0, :]] + [w_s1[:, t, :] for t in range(PACK - 1)]
+        xb_s = gather(xt_plane, U8, l1, FIRST, J, "xb_s")
         acc = bank(1, (PACK - 1) * FIRST)
         for t in range(1, PACK):
-            product(acc[:, (t - 1) * FIRST : t * FIRST], wd[t], sd[t], xa_w[:], xa_s[:], FP4X4)
+            product(acc[:, (t - 1) * FIRST : t * FIRST], w_wd[:, t, :], w_sd[:, t, :], xa_w[:], xa_s[:], FP4X4)
         a_first = new([P, (PACK - 1) * FIRST], F32, "a_first")
         nc.vector.tensor_copy(a_first[:], acc[:])
+        xb_w = gather(xt_w, U16, l1, FIRST, J, "xb_w", "xa_w")
+        pw.append(cleared_board(nc.vector, C, "pw3", "xa_s"))
         for t in range(1, PACK):
             scatter(pw[t], l3, 0, FIRST, a_first[:, (t - 1) * FIRST : t * FIRST])
 
         rest = J - FIRST
-        xb_s = gather(xt_plane, U8, l1, FIRST, J, "xb_s")
-        xb_w = gather(xt_w, U16, l1, FIRST, J, "xb_w")
-        for half in range(2):
-            acc = bank(2 + half, 2 * rest)
-            for i in range(2):
-                t = 2 * half + i
-                product(acc[:, i * rest : (i + 1) * rest], wd[t], sd[t], xb_w[:], xb_s[:], FP4X4)
-            a_rest = new([P, 2 * rest], F32, "a_rest%d" % half)
+        for t in range(PACK):
+            acc = bank(2 + t, rest)
+            product(acc[:], w_wd[:, t, :], w_sd[:, t, :], xb_w[:], xb_s[:], FP4X4)
+            a_rest = new([P, rest], F32, "a_rest%d" % t)
             nc.vector.tensor_copy(a_rest[:], acc[:])
-            for i in range(2):
-                scatter(pw[2 * half + i], l3, FIRST, J, a_rest[:, i * rest : (i + 1) * rest])
+            scatter(pw[t], l3, FIRST, J, a_rest[:])
 
-        xo_plane = cleared_plane(T, "xo_plane")
-        w2_plane = cleared_plane(R, "w2_plane")
-        wb_plane = cleared_plane(N, "wb_plane")
+        xo_plane = cleared_plane(nc.gpsimd, T, "xo_plane", "a_first0")
+        w2_plane = cleared_plane(nc.gpsimd, R, "w2_plane", "xb_s")
+        wb_plane = cleared_plane(nc.gpsimd, N, "wb_plane", "a_first")
         l2 = load_list(offs2, "l2")
         xo_w = load_fp4_words(xo_words, "xo_w")
         load_scales(xo_plane, xo_scales)
@@ -150,17 +144,17 @@ def tile_picked_tokens_plain_two_trailing_one_endsteps_kernel(
 
         xo_gs = gather(xo_plane, U8, l2, 0, J, "xo_g_s")
         xo_gw = gather(xo_w, U16, l2, 0, J, "xo_g_w")
-        w2_sd = deal(w2_plane, U8, 0, PACK, "w2_sd")
-        w2_wd = deal(w2_w, U32, 0, PACK, "w2_wd")
-        pv = [cleared_board(nc.gpsimd, C, "pv%d" % t, tag) for t, tag in enumerate(("xt_w", "xt_plane", "xo_w", "xo_plane"))]
+        w2_sd = deal(w2_plane, U8, "w2_sd")
+        w2_wd = deal(w2_w, U32, "w2_wd")
+        pv = [cleared_board(nc.gpsimd, C, "pv%d" % t, tag) for t, tag in enumerate(("xt_w", "xt_plane", "xo_w", "a_first0"))]
         for t in range(PACK):
-            acc = bank(4 + t, J)
+            acc = bank((6 + t) % 8, J)
             for lo, hi in ((0, 256), (256, J)):
                 product(acc[:, lo:hi], w2_wd[:, t, :], w2_sd[:, t, :], xo_gw[:, lo:hi], xo_gs[:, lo:hi], FP4X4)
             b_t = new([P, J], F32, "b%d" % t)
             nc.vector.tensor_copy(b_t[:], acc[:])
             scatter(pv[t], l4, 0, J, b_t[:])
-        m0 = [cleared_board(nc.gpsimd, U, "m0_%d" % j, tag) for j, tag in enumerate(("w2_w", "w2_plane"))]
+        m0 = [cleared_board(nc.gpsimd, U, "m0_%d" % j, tag) for j, tag in enumerate(("w2_w", "xb_s"))]
 
         g3 = []
         for t in range(PACK):
@@ -178,10 +172,17 @@ def tile_picked_tokens_plain_two_trailing_one_endsteps_kernel(
             for k, (lo, hi) in enumerate(C_CHUNKS):
                 nc.vector.tensor_tensor(woven[k][:, :, t], g3[t][:, lo:hi], pv[t][:, lo:hi], MAX)
 
+        split = C_CHUNKS[0][1]
+        nc.vector.tensor_tensor(woven[0][:, :, last], g3[last][:, 0:split], pv[last][:, 0:split], MAX)
+        hid_last = new([P, C - split], BF16, "hid_last")
+        nc.vector.tensor_tensor(hid_last[:], g3[last][:, split:C], pv[last][:, split:C], MAX)
         banks_used = 0
         for k, (lo, hi) in enumerate(C_CHUNKS):
             width = hi - lo
-            nc.vector.tensor_tensor(woven[k][:, :, last], g3[last][:, lo:hi], pv[last][:, lo:hi], MAX)
+            if k in (1, 2):
+                nc.scalar.copy(woven[k][:, :, last], hid_last[:, lo - split : hi - split])
+            elif k == 3:
+                nc.vector.tensor_copy(woven[k][:, :, last], hid_last[:, lo - split : hi - split])
             hid_w = new([P, width], U32, "hid_w%d" % k)
             hid_s = new([P, width], U8, "hid_s%d" % k)
             nc.vector.quantize_mx(out=hid_w[:].bitcast(FP8X4), scales=hid_s[:], in_=woven[k][:].rearrange("p c t -> p (c t)"))

from contextlib import ExitStack

import concourse.mybir as mybir

F32 = mybir.dt.float32
BF16 = mybir.dt.bfloat16
I32 = mybir.dt.int32
U32 = mybir.dt.uint32
U16 = mybir.dt.uint16
U8 = mybir.dt.uint8
FP8X4 = mybir.dt.float8_e4m3fn_x4
FP4X4 = mybir.dt.float4_e2m1fn_x4
ADD = mybir.AluOpType.add
SUB = mybir.AluOpType.subtract
MAX = mybir.AluOpType.max
COPY = mybir.ActivationFunctionType.Copy

P = 128
PACK = 4
J, R, T, C, N, U = 384, 512, 1024, 512, 256, 1024
FIRST = 128
C_CHUNKS = ((0, 64), (64, 128), (128, 256), (256, 512))
U_CHUNKS = (((0, 512), (512, 1024)), ((0, 128), (128, 384), (384, 640), (640, 896), (896, 1024)))
FLOPS = 2 * 512 * R * J * 2 + 2 * R * N * C


def tile_picked_tokens_plain_two_trailing_one_endsteps_kernel(
    tc, xt_words, xt_scales, w_words, w_scales, xo_words, xo_scales, w2_words, w2_scales,
    wb_words, wb_scales, offs, offs2, offs3, offs4, offs5, out,
):
    nc = tc.nc
    with ExitStack() as ctx:
        lists = ctx.enter_context(tc.tile_pool(name="lists", bufs=1))
        sb = ctx.enter_context(tc.tile_pool(name="sb", bufs=1))
        ps = ctx.enter_context(tc.psum_pool(name="ps", bufs=1))

        def new(shape, dtype, name, tag=None):
            return sb.tile(shape, dtype, name=name, tag=tag or name, align_bytes=64)

        def bank(index, width):
            return ps.tile([P, width], F32, name="bank%d" % index)

        def load_list(source, name):
            tile = lists.tile(list(source.shape), U16, name=name)
            nc.sync.dma_start(tile[:], source)
            return tile

        def load_fp4_words(source, name):
            tile = new([P, T], U16, name)
            nc.sync.dma_start(tile[:].bitcast(I32), source[0].bitcast(I32))
            return tile

        def load_fp8_words(source, name):
            tile = new([P, source.shape[2]], U32, name)
            nc.sync.dma_start(tile[:].bitcast(I32), source[0].rearrange("p n t -> p (n t)").bitcast(I32))
            return tile

        def cleared_plane(engine, width, name, tag=None):
            tile = new([P, width], U8, name, tag)
            engine.memset(tile[:].bitcast(I32), 0)
            return tile

        def load_scales(plane, source):
            for q in range(4):
                nc.sync.dma_start(plane[32 * q : 32 * q + 4, :].bitcast(I32), source[0, 4 * q : 4 * q + 4, :].bitcast(I32))

        def cleared_board(engine, width, name, tag=None):
            tile = new([P, width], F32, name, tag)
            engine.memset(tile[:].bitcast(I32), 0)
            return tile

        def gather(window, dtype, offsets, lo, hi, name, tag=None):
            tile = new([P, hi - lo], dtype, name, tag)
            nc.vector.tensor_copy(tile[:], window[:].indirect(offsets[:, lo // 16 : hi // 16]))
            return tile

        def deal(source, dtype, name):
            tile = new([P, PACK, P], dtype, name)
            nc.vector.tensor_copy(tile[:], source[:].rearrange("p (m t) -> p t m", t=PACK))
            return tile

        def product(acc, wt_words, wt_scales, moving, moving_scales, fmt):
            nc.tensor.matmul_mx(out=acc, lhsT=wt_words.bitcast(FP8X4), lhsT_scale=wt_scales,
                                rhs=moving.bitcast(fmt), rhs_scale=moving_scales, start=True, stop=True)

        def scatter(board, offsets, lo, hi, values):
            nc.scalar.activation(board[:].indirect(offsets[:, lo // 16 : hi // 16]), values, COPY)

        xt_plane = cleared_plane(nc.vector, T, "xt_plane")
        w_plane = cleared_plane(nc.vector, R, "w_plane")
        w_stage = new([4, 4, R // 4], I32, "w_stage")
        nc.sync.dma_start(w_stage[:], w_scales[0].bitcast(I32).rearrange("(q r) c -> r q c", r=4))
        l1 = load_list(offs, "l1")
        xt_w = load_fp4_words(xt_words, "xt_w")
        w_w = load_fp8_words(w_words, "w_w")
        load_scales(xt_plane, xt_scales)
        l3 = load_list(offs3, "l3")
        pw = [cleared_board(nc.vector, C, "pw%d" % t) for t in range(PACK - 1)]

        for q in range(4):
            nc.vector.tensor_copy(w_plane[32 * q : 32 * q + 4, :].bitcast(I32), w_stage[:, q, :])
        w_wd = new([P, PACK, P], U32, "w_wd")
        nc.scalar.copy(w_wd[:].rearrange("p t m -> p m t"), w_w[:].rearrange("p (m t) -> p m t", t=PACK))
        w_sd = deal(w_plane, U8, "w_sd")
        xa_w = gather(xt_w, U16, l1, 0, FIRST, "xa_w")
        xa_s = gather(xt_plane, U8, l1, 0, FIRST, "xa_s")
        acc = bank(0, FIRST)
        product(acc[:], w_wd[:, 0, :], w_sd[:, 0, :], xa_w[:], xa_s[:], FP4X4)
        a_first0 = new([P, FIRST], F32, "a_first0")
        nc.scalar.copy(a_first0[:], acc[:])
        scatter(pw[0], l3, 0, FIRST, a_first0[:])

        xb_s = gather(xt_plane, U8, l1, FIRST, J, "xb_s")
        acc = bank(1, (PACK - 1) * FIRST)
        for t in range(1, PACK):
            product(acc[:, (t - 1) * FIRST : t * FIRST], w_wd[:, t, :], w_sd[:, t, :], xa_w[:], xa_s[:], FP4X4)
        a_first = new([P, (PACK - 1) * FIRST], F32, "a_first")
        nc.vector.tensor_copy(a_first[:], acc[:])
        xb_w = gather(xt_w, U16, l1, FIRST, J, "xb_w", "xa_w")
        pw.append(cleared_board(nc.vector, C, "pw3", "xa_s"))
        for t in range(1, PACK):
            scatter(pw[t], l3, 0, FIRST, a_first[:, (t - 1) * FIRST : t * FIRST])

        rest = J - FIRST
        for t in range(PACK):
            acc = bank(2 + t, rest)
            product(acc[:], w_wd[:, t, :], w_sd[:, t, :], xb_w[:], xb_s[:], FP4X4)
            a_rest = new([P, rest], F32, "a_rest%d" % t)
            nc.vector.tensor_copy(a_rest[:], acc[:])
            scatter(pw[t], l3, FIRST, J, a_rest[:])

        xo_plane = cleared_plane(nc.gpsimd, T, "xo_plane", "a_first0")
        w2_plane = cleared_plane(nc.gpsimd, R, "w2_plane", "xb_s")
        wb_plane = cleared_plane(nc.gpsimd, N, "wb_plane", "a_first")
        l2 = load_list(offs2, "l2")
        xo_w = load_fp4_words(xo_words, "xo_w")
        load_scales(xo_plane, xo_scales)
        w2_w = load_fp8_words(w2_words, "w2_w")
        load_scales(w2_plane, w2_scales)
        l4 = load_list(offs4, "l4")
        wb_w = load_fp8_words(wb_words, "wb_w")
        load_scales(wb_plane, wb_scales)
        l5 = load_list(offs5, "l5")

        xo_gs = gather(xo_plane, U8, l2, 0, J, "xo_g_s")
        xo_gw = gather(xo_w, U16, l2, 0, J, "xo_g_w")
        w2_sd = deal(w2_plane, U8, "w2_sd")
        w2_wd = deal(w2_w, U32, "w2_wd")
        pv = [cleared_board(nc.gpsimd, C, "pv%d" % t, tag) for t, tag in enumerate(("xt_w", "xt_plane", "xo_w", "a_first0"))]
        for t in range(PACK):
            acc = bank((6 + t) % 8, J)
            for lo, hi in ((0, 256), (256, J)):
                product(acc[:, lo:hi], w2_wd[:, t, :], w2_sd[:, t, :], xo_gw[:, lo:hi], xo_gs[:, lo:hi], FP4X4)
            b_t = new([P, J], F32, "b%d" % t)
            nc.vector.tensor_copy(b_t[:], acc[:])
            scatter(pv[t], l4, 0, J, b_t[:])
        m0 = [cleared_board(nc.gpsimd, U, "m0_%d" % j, tag) for j, tag in enumerate(("w2_w", "xb_s"))]

        g3 = []
        for t in range(PACK):
            g1 = new([P, 2 + C], F32, "g1_%d" % t, ("xo_g_w", "xo_g_s", "w2_wd", "w2_sd")[t])
            nc.vector.memset(g1[:, 0:2], 0.0)
            nc.vector.tensor_copy(g1[:, 2:3], pw[t][:, 0:1])
            nc.vector.tensor_tensor(g1[:, 3 : 2 + C], pw[t][:, 1:C], pw[t][:, 0 : C - 1], ADD)
            g3_t = new([P, C], F32, "g3_%d" % t)
            nc.vector.tensor_tensor(g3_t[:], g1[:, 2 : 2 + C], g1[:, 0:C], ADD)
            g3.append(g3_t)

        last = PACK - 1
        woven = [new([P, hi - lo, PACK], BF16, "woven%d" % k) for k, (lo, hi) in enumerate(C_CHUNKS)]
        for t in range(last):
            for k, (lo, hi) in enumerate(C_CHUNKS):
                nc.vector.tensor_tensor(woven[k][:, :, t], g3[t][:, lo:hi], pv[t][:, lo:hi], MAX)

        split = C_CHUNKS[0][1]
        nc.vector.tensor_tensor(woven[0][:, :, last], g3[last][:, 0:split], pv[last][:, 0:split], MAX)
        hid_last = new([P, C - split], BF16, "hid_last")
        nc.vector.tensor_tensor(hid_last[:], g3[last][:, split:C], pv[last][:, split:C], MAX)
        banks_used = 0
        for k, (lo, hi) in enumerate(C_CHUNKS):
            width = hi - lo
            if k in (1, 2):
                nc.scalar.copy(woven[k][:, :, last], hid_last[:, lo - split : hi - split])
            elif k == 3:
                nc.vector.tensor_copy(woven[k][:, :, last], hid_last[:, lo - split : hi - split])
            hid_w = new([P, width], U32, "hid_w%d" % k)
            hid_s = new([P, width], U8, "hid_s%d" % k)
            nc.vector.quantize_mx(out=hid_w[:].bitcast(FP8X4), scales=hid_s[:], in_=woven[k][:].rearrange("p c t -> p (c t)"))
            groups = ((0,), (1,)) if width < P else ((0, 1),)
            sources = []
            for group in groups:
                acc = bank(banks_used, len(group) * width)
                banks_used = banks_used + 1
                for i, j in enumerate(group):
                    product(acc[:, i * width : (i + 1) * width], wb_w[:, j * P : (j + 1) * P],
                            wb_plane[:, j * P : (j + 1) * P], hid_w[:], hid_s[:], FP8X4)
                p_k = new([P, len(group) * width], F32, "p%d_%d" % (k, group[0]))
                if k == 0:
                    nc.scalar.copy(p_k[:], acc[:])
                else:
                    nc.vector.tensor_copy(p_k[:], acc[:])
                sources.extend(p_k[:, i * width : (i + 1) * width] for i in range(len(group)))
            for j in range(N // P):
                scatter(m0[j], l5, lo, hi, sources[j])

        for j in range(N // P):
            for lo, hi in U_CHUNKS[j]:
                y = new([P, hi - lo], F32, "y%d_%d" % (j, lo))
                if lo == 0:
                    nc.vector.tensor_copy(y[:, 0:1], m0[j][:, 0:1])
                    nc.vector.tensor_tensor(y[:, 1:], m0[j][:, 1:hi], m0[j][:, 0 : hi - 1], SUB)
                else:
                    nc.vector.tensor_tensor(y[:], m0[j][:, lo:hi], m0[j][:, lo - 1 : hi - 1], SUB)
                nc.sync.dma_start(out[j * P : (j + 1) * P, lo:hi], y[:])
